import numpy as np
import ml_dtypes


def mxq(x, axis, fmt="e4m3"):
    dtype, down = {"e4m3": (ml_dtypes.float8_e4m3fn, 7), "e5m2": (ml_dtypes.float8_e5m2, 14)}[fmt]
    v = np.moveaxis(np.asarray(x, np.float32).astype(ml_dtypes.bfloat16).astype(np.float64), axis, -1)
    blocks = v.reshape(v.shape[:-1] + (-1, 32))
    amax = np.abs(blocks).max(-1, keepdims=True)
    byte = np.maximum(np.where(amax > 0, np.frexp(amax)[1] - 1 + 127, 0) - down, 1)
    scale = np.exp2(byte - 127.0)
    codes = (blocks / scale).astype(np.float32).astype(dtype).astype(np.float64)
    return np.moveaxis((codes * scale).reshape(v.shape), -1, axis)


WIDE = False


def mx_kscale(k):
    if not WIDE:
        return np.ones(k)
    levels = np.array([30, -30])
    if k % 512:
        return np.exp2(np.random.permutation(np.resize(levels, k // 32))).repeat(32)
    a = np.empty((k // 512, 16))
    for p in range(k // 512):
        a[p, :8] = np.random.permutation(np.resize(levels, 8))
        for g in range(8):
            far = levels[np.abs(levels - a[p, g]) >= 10]
            a[p, g + 8] = far[np.random.randint(len(far))]
    return np.exp2(a.ravel()).repeat(32)


def f64(x):
    return np.asarray(x).astype(np.float64)


def striped(idx):
    return np.tile(np.asarray(idx).reshape(-1, 16).T, (8, 1)).astype(np.uint16)


def unstriped(offs):
    return offs[:16].T.reshape(-1).astype(np.int64)


E2M1 = np.array([0.0, 0.5, 1.0, 1.5, 2.0, 3.0, 4.0, 6.0, -0.0, -0.5, -1.0, -1.5, -2.0, -3.0, -4.0, -6.0])


def pack_weight(w, fmt):
    k, n = w.shape
    w = f64(np.asarray(w, np.float32).astype(ml_dtypes.bfloat16)).reshape(k // 32, 32, n)
    amax = np.abs(w).max(1)
    if fmt in ("e4m3", "e5m2"):
        byte = np.frexp(amax)[1] - 1 + 127 - (7 if fmt == "e4m3" else 14)
    else:
        mant, ex = np.frexp(amax / 6.0)
        byte = np.where(mant > 0.5, ex, ex - 1) + 127
    byte = np.clip(np.where(amax > 0, byte, 1), 1, 254)
    scaled = (w * np.exp2(127.0 - byte)[:, None, :]).reshape(k, n).astype(np.float32)
    by_word = np.ascontiguousarray(scaled.reshape(k // 512, 128, 4, n).transpose(0, 1, 3, 2))
    if fmt in ("e4m3", "e5m2"):
        words = by_word.astype(ml_dtypes.float8_e4m3fn if fmt == "e4m3" else ml_dtypes.float8_e5m2).view(np.uint8)
    else:
        c = by_word.astype(ml_dtypes.float4_e2m1fn).view(np.uint8) & 0xF
        words = (c[..., 0::2] | (c[..., 1::2] << 4)).reshape(k // 512, 128, 2 * n)
    return np.ascontiguousarray(words), np.ascontiguousarray(byte.astype(np.uint8).reshape(k // 512, 16, n))


def unpack_weight(words, scales, fmt):
    g, _, n = scales.shape
    words = np.ascontiguousarray(words).reshape(g, 128, n, -1)
    if fmt in ("e4m3", "e5m2"):
        vals = words.view(ml_dtypes.float8_e4m3fn if fmt == "e4m3" else ml_dtypes.float8_e5m2).astype(np.float64)
    else:
        nib = np.empty((g, 128, n, 4), np.uint8)
        nib[..., 0::2] = words & 0xF
        nib[..., 1::2] = words >> 4
        vals = E2M1[nib]
    vals = vals * np.repeat(np.exp2(scales.astype(np.float64) - 127.0), 8, axis=1)[..., None]
    return vals.transpose(0, 1, 3, 2).reshape(g * 512, n)


K, T, I, J, N, Z, S, V, E = 512, 1024, 512, 256, 256, 1024, 1024, 1024, 128


def setup_inputs():
    n = np.random.standard_normal
    idx = np.random.permutation(T)[:I]
    idx2 = np.random.permutation(Z)[:J]
    idx3 = np.random.permutation(V)[:J]
    idx4 = np.random.permutation(S)[:N]
    idx5 = np.random.permutation(J)[:E]
    idx6 = np.random.permutation(J)[:E]
    fk = mx_kscale(K)
    fi = mx_kscale(I)
    ti = np.ones(T)
    ti[idx] = fi
    xkp = pack_weight(n((K, T)) * 0.3 * fk[:, None] * ti, "e4m3")
    xqp = pack_weight(n((K, Z)) * 0.3 / fk[:, None], "e2m1")
    xrp = pack_weight(n((K, V)) * 0.3 / fk[:, None], "e5m2")
    vsp = pack_weight(n((I, S)) / fi[:, None], "e2m1")
    return {
        "xk_words": xkp[0],
        "xk_scales": xkp[1],
        "xq_words": xqp[0],
        "xq_scales": xqp[1],
        "xr_words": xrp[0],
        "xr_scales": xrp[1],
        "vs_words": vsp[0],
        "vs_scales": vsp[1],
        "offs": striped(idx),
        "offs2": striped(idx2),
        "offs3": striped(idx3),
        "offs4": striped(idx4),
        "offs5": striped(idx5),
        "offs6": striped(idx6),
    }


def reference(xk_words, xk_scales, xq_words, xq_scales, xr_words, xr_scales, vs_words, vs_scales, offs, offs2, offs3, offs4, offs5, offs6):
    idx = unstriped(offs)
    idx2 = unstriped(offs2)
    idx3 = unstriped(offs3)
    idx4 = unstriped(offs4)
    idx5 = unstriped(offs5)
    idx6 = unstriped(offs6)
    xku = unpack_weight(xk_words, xk_scales, "e4m3")
    xqu = unpack_weight(xq_words, xq_scales, "e2m1")
    xru = unpack_weight(xr_words, xr_scales, "e5m2")
    vsu = unpack_weight(vs_words, vs_scales, "e2m1")
    xkidxg = xku[:, idx]
    xqidx2g = xqu[:, idx2]
    s1 = xkidxg.T @ xqidx2g
    xridx3g = xru[:, idx3]
    s2 = xkidxg.T @ xridx3g
    hid = np.abs(s1 - s2)
    vsidx4g = vsu[:, idx4]
    hidq = mxq(hid, 0, "e4m3")
    p = vsidx4g.T @ hidq
    y = np.maximum(p[:, idx5], p[:, idx6])
    return y

@@ -1,0 +1,153 @@
+from contextlib import ExitStack
+
+import concourse.mybir as mybir
+
+K, T, I, J, N, E = 512, 1024, 512, 256, 256, 128
+FLOPS = 2 * K * I * J * 2 + 2 * I * N * J
+
+F32 = mybir.dt.float32
+BF16 = mybir.dt.bfloat16
+I32 = mybir.dt.int32
+U32 = mybir.dt.uint32
+U16 = mybir.dt.uint16
+U8 = mybir.dt.uint8
+E4M3 = mybir.dt.float8_e4m3fn_x4
+E5M2 = mybir.dt.float8_e5m2_x4
+E2M1 = mybir.dt.float4_e2m1fn_x4
+ACT = mybir.ActivationFunctionType
+ALU = mybir.AluOpType
+
+P = 128
+PACK = 4
+HALF = 128
+
+
+def tile_list_contest_rivals_direct_bestoftwo_kernel(
+    tc, xk_words, xk_scales, xq_words, xq_scales, xr_words, xr_scales, vs_words, vs_scales,
+    offs, offs2, offs3, offs4, offs5, offs6, out,
+):
+    nc = tc.nc
+    with ExitStack() as ctx:
+        held = ctx.enter_context(tc.tile_pool(name="held", bufs=1))
+        psum = ctx.enter_context(tc.psum_pool(name="psum", bufs=1))
+
+        def load_list(name, src):
+            tile = held.tile(list(src.shape), U16, name=name)
+            nc.sync.dma_start(tile[:], src)
+            return tile
+
+        def load_words(name, src, dtype, queue):
+            tile = held.tile([P, T], dtype, name=name, align_bytes=64)
+            queue.dma_start(tile[:].bitcast(I32), src.bitcast(I32))
+            return tile
+
+        def zeroed_scale_tile(name, engine):
+            tile = held.tile([P, T], U8, name=name, align_bytes=64)
+            engine.memset(tile[:].bitcast(I32), 0)
+            return tile
+
+        def load_scales(tile, src, queue):
+            for q in range(4):
+                queue.dma_start(tile[32 * q : 32 * q + 4, :].bitcast(I32), src[0, 4 * q : 4 * q + 4, :].bitcast(I32))
+
+        def gather(name, table, entries, count, dtype):
+            tile = held.tile([P, count], dtype, name=name, align_bytes=64)
+            nc.vector.tensor_copy(tile[:], table[:].indirect(entries[:]))
+            return tile
+
+        def gather_dealt(name, table, entries, dtype):
+            tile = held.tile([P, I], dtype, name=name, align_bytes=64)
+            nc.vector.tensor_copy(tile[:].rearrange("p (t m) -> p m t", t=PACK), table[:].indirect(entries[:]))
+            return tile
+
+        q_scale_tab = zeroed_scale_tile("q_scale_tab", nc.vector)
+        k_scale_tab = zeroed_scale_tile("k_scale_tab", nc.gpsimd)
+        r_scale_tab = zeroed_scale_tile("r_scale_tab", nc.vector)
+        v_scale_tab = zeroed_scale_tile("v_scale_tab", nc.gpsimd)
+
+        q_list = load_list("q_list", offs2)
+        q_word_tab = load_words("q_word_tab", xq_words[0], U16, nc.scalar)
+        load_scales(q_scale_tab, xq_scales, nc.sync)
+        k_list = load_list("k_list", offs)
+        k_word_tab = load_words("k_word_tab", xk_words[0].rearrange("p c r -> p (c r)"), U32, nc.scalar)
+        load_scales(k_scale_tab, xk_scales, nc.sync)
+        r_list = load_list("r_list", offs3)
+        r_word_tab = load_words("r_word_tab", xr_words[0].rearrange("p c r -> p (c r)"), U32, nc.sync)
+        load_scales(r_scale_tab, xr_scales, nc.sync)
+        v_list = load_list("v_list", offs4)
+        v_word_tab = load_words("v_word_tab", vs_words[0], U16, nc.sync)
+        load_scales(v_scale_tab, vs_scales, nc.sync)
+        first_list = load_list("first_list", offs5)
+        second_list = load_list("second_list", offs6)
+
+        q_words = gather("q_words", q_word_tab, q_list, J, U16)
+        q_scales = gather("q_scales", q_scale_tab, q_list, J, U8)
+        k_words = gather_dealt("k_words", k_word_tab, k_list, U32)
+        k_scales = gather_dealt("k_scales", k_scale_tab, k_list, U8)
+
+        def scores(name, words, scales, dtype, h):
+            bank = psum.tile([P, PACK, HALF], F32, name=name)
+            cols = slice(h * HALF, (h + 1) * HALF)
+            for t in range(PACK):
+                rows = slice(t * P, (t + 1) * P)
+                nc.tensor.matmul_mx(
+                    out=bank[:, t, :],
+                    lhsT=k_words[:, rows].bitcast(E4M3), lhsT_scale=k_scales[:, rows],
+                    rhs=words[:, cols].bitcast(dtype), rhs_scale=scales[:, cols],
+                    start=True, stop=True,
+                )
+            return bank
+
+        s1 = []
+        for h in range(2):
+            bank = scores("s1_bank%d" % h, q_words, q_scales, E2M1, h)
+            tile = held.tile([P, HALF, PACK], F32, name="s1_%d" % h)
+            nc.scalar.copy(tile[:], bank[:].rearrange("p t j -> p j t"))
+            s1.append(tile)
+
+        r_words = gather("r_words", r_word_tab, r_list, J, U32)
+        r_scales = gather("r_scales", r_scale_tab, r_list, J, U8)
+        v_words = gather("v_words", v_word_tab, v_list, N, U16)
+
+        hid = []
+        for h in range(2):
+            bank = scores("s2_bank%d" % h, r_words, r_scales, E5M2, h)
+            diff = held.tile([P, HALF, PACK], F32, name="diff%d" % h)
+            nc.vector.tensor_tensor(diff[:], s1[h][:], bank[:].rearrange("p t j -> p j t"), ALU.subtract)
+            rounded = held.tile([P, HALF * PACK], BF16, name="hid%d" % h, align_bytes=64)
+            nc.scalar.activation(rounded[:], diff[:].rearrange("p j t -> p (j t)"), ACT.Abs)
+            hid.append(rounded)
+
+        v_scales = gather("v_scales", v_scale_tab, v_list, N, U8)
+
+        p_tiles = [held.tile([P, J], F32, name="p%d" % b) for b in range(2)]
+        for h in range(2):
+            codes = held.tile([P, HALF], U32, name="hid_words%d" % h, align_bytes=64)
+            scales = held.tile([P, HALF], U8, name="hid_scales%d" % h, align_bytes=64)
+            nc.vector.quantize_mx(out=codes[:].bitcast(E4M3), scales=scales[:], in_=hid[h][:])
+            for b in range(2):
+                rows = slice(b * P, (b + 1) * P)
+                bank = psum.tile([P, HALF], F32, name="p_bank%d%d" % (h, b))
+                nc.tensor.matmul_mx(
+                    out=bank[:],
+                    lhsT=v_words[:, rows].bitcast(E2M1), lhsT_scale=v_scales[:, rows],
+                    rhs=codes[:].bitcast(E4M3), rhs_scale=scales[:],
+                    start=True, stop=True,
+                )
+                dst = p_tiles[b][:, h * HALF : (h + 1) * HALF]
+                if h == 1 and b == 0:
+                    nc.vector.tensor_copy(dst, bank[:])
+                else:
+                    nc.scalar.copy(dst, bank[:])
+
+        for b in range(2):
+            first = held.tile([P, E], F32, name="first%d" % b)
+            second = held.tile([P, E], F32, name="second%d" % b)
+            for tile, entries in ((first, first_list), (second, second_list)):
+                if b == 0:
+                    nc.vector.tensor_copy(tile[:], p_tiles[b][:].indirect(entries[:]))
+                else:
+                    nc.scalar.activation(tile[:], p_tiles[b][:].indirect(entries[:]), ACT.Copy)
+            best = held.tile([P, E], F32, name="best%d" % b)
+            nc.vector.tensor_tensor(best[:], first[:], second[:], ALU.max)
+            nc.sync.dma_start(out[b * P : (b + 1) * P, :], best[:])

@@ -37,53 +37,62 @@ def tile_list_contest_rivals_direct_bestoftwo_kernel(
             return tile
 
         def load_words(name, src, dtype, queue):
-            tile = held.tile([P, T], dtype, name=name, align_bytes=64)
+            tile = held.tile([P, T], dtype, name=name, tag=name, align_bytes=64)
             queue.dma_start(tile[:].bitcast(I32), src.bitcast(I32))
             return tile
 
         def zeroed_scale_tile(name, engine):
-            tile = held.tile([P, T], U8, name=name, align_bytes=64)
+            tile = held.tile([P, T], U8, name=name, tag=name, align_bytes=64)
             engine.memset(tile[:].bitcast(I32), 0)
             return tile
 
-        def load_scales(tile, src, queue):
+        def load_scales(tile, src, queues):
             for q in range(4):
-                queue.dma_start(tile[32 * q : 32 * q + 4, :].bitcast(I32), src[0, 4 * q : 4 * q + 4, :].bitcast(I32))
+                queues[q].dma_start(tile[32 * q : 32 * q + 4, :].bitcast(I32), src[0, 4 * q : 4 * q + 4, :].bitcast(I32))
 
         def gather(name, table, entries, count, dtype):
             tile = held.tile([P, count], dtype, name=name, align_bytes=64)
             nc.vector.tensor_copy(tile[:], table[:].indirect(entries[:]))
             return tile
 
+        def gather_halves(name, word_tab, scale_tab, entries, dtype):
+            words = held.tile([P, J], dtype, name=name + "_words", align_bytes=64)
+            scales = held.tile([P, J], U8, name=name + "_scales", align_bytes=64)
+            for h in range(2):
+                cols = slice(h * HALF, (h + 1) * HALF)
+                part = entries[:, h * HALF // 16 : (h + 1) * HALF // 16]
+                nc.vector.tensor_copy(words[:, cols], word_tab[:].indirect(part))
+                nc.vector.tensor_copy(scales[:, cols], scale_tab[:].indirect(part))
+            return words, scales
+
         def gather_dealt(name, table, entries, dtype):
             tile = held.tile([P, I], dtype, name=name, align_bytes=64)
             nc.vector.tensor_copy(tile[:].rearrange("p (t m) -> p m t", t=PACK), table[:].indirect(entries[:]))
             return tile
 
+        k_scale_tab = zeroed_scale_tile("k_scale_tab", nc.vector)
         q_scale_tab = zeroed_scale_tile("q_scale_tab", nc.vector)
-        k_scale_tab = zeroed_scale_tile("k_scale_tab", nc.gpsimd)
-        r_scale_tab = zeroed_scale_tile("r_scale_tab", nc.vector)
+        r_scale_tab = zeroed_scale_tile("r_scale_tab", nc.gpsimd)
         v_scale_tab = zeroed_scale_tile("v_scale_tab", nc.gpsimd)
 
-        q_list = load_list("q_list", offs2)
-        q_word_tab = load_words("q_word_tab", xq_words[0], U16, nc.scalar)
-        load_scales(q_scale_tab, xq_scales, nc.sync)
         k_list = load_list("k_list", offs)
-        k_word_tab = load_words("k_word_tab", xk_words[0].rearrange("p c r -> p (c r)"), U32, nc.scalar)
-        load_scales(k_scale_tab, xk_scales, nc.sync)
-        r_list = load_list("r_list", offs3)
+        load_scales(k_scale_tab, xk_scales, (nc.sync, nc.scalar, nc.sync, nc.scalar))
+        k_word_tab = load_words("k_word_tab", xk_words[0].rearrange("p c r -> p (c r)"), U32, nc.sync)
+        q_word_tab = load_words("q_word_tab", xq_words[0], U16, nc.sync)
+        load_scales(q_scale_tab, xq_scales, (nc.sync,) * 4)
+        q_list = load_list("q_list", offs2)
         r_word_tab = load_words("r_word_tab", xr_words[0].rearrange("p c r -> p (c r)"), U32, nc.sync)
-        load_scales(r_scale_tab, xr_scales, nc.sync)
-        v_list = load_list("v_list", offs4)
+        load_scales(r_scale_tab, xr_scales, (nc.sync,) * 4)
+        r_list = load_list("r_list", offs3)
         v_word_tab = load_words("v_word_tab", vs_words[0], U16, nc.sync)
-        load_scales(v_scale_tab, vs_scales, nc.sync)
+        load_scales(v_scale_tab, vs_scales, (nc.sync,) * 4)
+        v_list = load_list("v_list", offs4)
         first_list = load_list("first_list", offs5)
         second_list = load_list("second_list", offs6)
 
-        q_words = gather("q_words", q_word_tab, q_list, J, U16)
-        q_scales = gather("q_scales", q_scale_tab, q_list, J, U8)
-        k_words = gather_dealt("k_words", k_word_tab, k_list, U32)
         k_scales = gather_dealt("k_scales", k_scale_tab, k_list, U8)
+        k_words = gather_dealt("k_words", k_word_tab, k_list, U32)
+        q_words, q_scales = gather_halves("q", q_word_tab, q_scale_tab, q_list, U16)
 
         def scores(name, words, scales, dtype, h):
             bank = psum.tile([P, PACK, HALF], F32, name=name)
@@ -105,37 +114,38 @@ def tile_list_contest_rivals_direct_bestoftwo_kernel(
             nc.scalar.copy(tile[:], bank[:].rearrange("p t j -> p j t"))
             s1.append(tile)
 
-        r_words = gather("r_words", r_word_tab, r_list, J, U32)
-        r_scales = gather("r_scales", r_scale_tab, r_list, J, U8)
-        v_words = gather("v_words", v_word_tab, v_list, N, U16)
+        r_words, r_scales = gather_halves("r", r_word_tab, r_scale_tab, r_list, U32)
 
         hid = []
+        diffs = held.tile([P, 2, HALF, PACK], F32, name="diffs")
         for h in range(2):
             bank = scores("s2_bank%d" % h, r_words, r_scales, E5M2, h)
-            diff = held.tile([P, HALF, PACK], F32, name="diff%d" % h)
-            nc.vector.tensor_tensor(diff[:], s1[h][:], bank[:].rearrange("p t j -> p j t"), ALU.subtract)
+            diff = diffs[:, h]
+            nc.vector.tensor_tensor(diff, s1[h][:], bank[:].rearrange("p t j -> p j t"), ALU.subtract)
             rounded = held.tile([P, HALF * PACK], BF16, name="hid%d" % h, align_bytes=64)
-            nc.scalar.activation(rounded[:], diff[:].rearrange("p j t -> p (j t)"), ACT.Abs)
+            nc.scalar.activation(rounded[:], diff.rearrange("p j t -> p (j t)"), ACT.Abs)
             hid.append(rounded)
 
+        v_words = gather("v_words", v_word_tab, v_list, N, U16)
         v_scales = gather("v_scales", v_scale_tab, v_list, N, U8)
 
+        codes_both = held.tile([P, 2, HALF], U32, name="hid_words", tag="v_word_tab", align_bytes=64)
         p_tiles = [held.tile([P, J], F32, name="p%d" % b) for b in range(2)]
         for h in range(2):
-            codes = held.tile([P, HALF], U32, name="hid_words%d" % h, align_bytes=64)
+            codes = codes_both[:, h]
             scales = held.tile([P, HALF], U8, name="hid_scales%d" % h, align_bytes=64)
-            nc.vector.quantize_mx(out=codes[:].bitcast(E4M3), scales=scales[:], in_=hid[h][:])
+            nc.vector.quantize_mx(out=codes.bitcast(E4M3), scales=scales[:], in_=hid[h][:])
             for b in range(2):
                 rows = slice(b * P, (b + 1) * P)
                 bank = psum.tile([P, HALF], F32, name="p_bank%d%d" % (h, b))
                 nc.tensor.matmul_mx(
                     out=bank[:],
                     lhsT=v_words[:, rows].bitcast(E2M1), lhsT_scale=v_scales[:, rows],
-                    rhs=codes[:].bitcast(E4M3), rhs_scale=scales[:],
+                    rhs=codes.bitcast(E4M3), rhs_scale=scales[:],
                     start=True, stop=True,
                 )
                 dst = p_tiles[b][:, h * HALF : (h + 1) * HALF]
-                if h == 1 and b == 0:
+                if b == 1:
                     nc.vector.tensor_copy(dst, bank[:])
                 else:
                     nc.scalar.copy(dst, bank[:])
@@ -144,7 +154,7 @@ def tile_list_contest_rivals_direct_bestoftwo_kernel(
             first = held.tile([P, E], F32, name="first%d" % b)
             second = held.tile([P, E], F32, name="second%d" % b)
             for tile, entries in ((first, first_list), (second, second_list)):
-                if b == 0:
+                if b == 1:
                     nc.vector.tensor_copy(tile[:], p_tiles[b][:].indirect(entries[:]))
                 else:
                     nc.scalar.activation(tile[:], p_tiles[b][:].indirect(entries[:]), ACT.Copy)

@@ -70,13 +70,17 @@ def tile_list_contest_rivals_direct_bestoftwo_kernel(
             nc.vector.tensor_copy(tile[:].rearrange("p (t m) -> p m t", t=PACK), table[:].indirect(entries[:]))
             return tile
 
-        k_scale_tab = zeroed_scale_tile("k_scale_tab", nc.vector)
         q_scale_tab = zeroed_scale_tile("q_scale_tab", nc.vector)
         r_scale_tab = zeroed_scale_tile("r_scale_tab", nc.gpsimd)
         v_scale_tab = zeroed_scale_tile("v_scale_tab", nc.gpsimd)
 
         k_list = load_list("k_list", offs)
-        load_scales(k_scale_tab, xk_scales, (nc.sync, nc.scalar, nc.sync, nc.scalar))
+        k_scale_tab = held.tile([P, T], U8, name="k_scale_tab", align_bytes=64)
+        for q in range(4):
+            rows = xk_scales[0, 4 * q : 4 * q + 4, :].bitcast(I32)
+            (nc.scalar, nc.sync)[q % 2].dma_start(
+                k_scale_tab[32 * q : 32 * q + 32, :].bitcast(I32), rows.unsqueeze(0).broadcast_to([8, 4, T // 4])
+            )
         k_word_tab = load_words("k_word_tab", xk_words[0].rearrange("p c r -> p (c r)"), U32, nc.sync)
         q_word_tab = load_words("q_word_tab", xq_words[0], U16, nc.sync)
         load_scales(q_scale_tab, xq_scales, (nc.sync,) * 4)
@@ -150,6 +154,7 @@ def tile_list_contest_rivals_direct_bestoftwo_kernel(
                 else:
                     nc.scalar.copy(dst, bank[:])
 
+        picked = []
         for b in range(2):
             first = held.tile([P, E], F32, name="first%d" % b)
             second = held.tile([P, E], F32, name="second%d" % b)
@@ -158,6 +163,8 @@ def tile_list_contest_rivals_direct_bestoftwo_kernel(
                     nc.vector.tensor_copy(tile[:], p_tiles[b][:].indirect(entries[:]))
                 else:
                     nc.scalar.activation(tile[:], p_tiles[b][:].indirect(entries[:]), ACT.Copy)
+            picked.append((first, second))
+        for b in (1, 0):
             best = held.tile([P, E], F32, name="best%d" % b)
-            nc.vector.tensor_tensor(best[:], first[:], second[:], ALU.max)
+            nc.vector.tensor_tensor(best[:], picked[b][0][:], picked[b][1][:], ALU.max)
             nc.sync.dma_start(out[b * P : (b + 1) * P, :], best[:])

from contextlib import ExitStack

import concourse.mybir as mybir

K, T, I, J, N, E = 512, 1024, 512, 256, 256, 128
FLOPS = 2 * K * I * J * 2 + 2 * I * N * J

F32 = mybir.dt.float32
BF16 = mybir.dt.bfloat16
I32 = mybir.dt.int32
U32 = mybir.dt.uint32
U16 = mybir.dt.uint16
U8 = mybir.dt.uint8
E4M3 = mybir.dt.float8_e4m3fn_x4
E5M2 = mybir.dt.float8_e5m2_x4
E2M1 = mybir.dt.float4_e2m1fn_x4
ACT = mybir.ActivationFunctionType
ALU = mybir.AluOpType

P = 128
PACK = 4
HALF = 128


def tile_list_contest_rivals_direct_bestoftwo_kernel(
    tc, xk_words, xk_scales, xq_words, xq_scales, xr_words, xr_scales, vs_words, vs_scales,
    offs, offs2, offs3, offs4, offs5, offs6, out,
):
    nc = tc.nc
    with ExitStack() as ctx:
        held = ctx.enter_context(tc.tile_pool(name="held", bufs=1))
        psum = ctx.enter_context(tc.psum_pool(name="psum", bufs=1))

        def load_list(name, src):
            tile = held.tile(list(src.shape), U16, name=name)
            nc.sync.dma_start(tile[:], src)
            return tile

        def load_words(name, src, dtype, queue):
            tile = held.tile([P, T], dtype, name=name, tag=name, align_bytes=64)
            queue.dma_start(tile[:].bitcast(I32), src.bitcast(I32))
            return tile

        def zeroed_scale_tile(name, engine):
            tile = held.tile([P, T], U8, name=name, tag=name, align_bytes=64)
            engine.memset(tile[:].bitcast(I32), 0)
            return tile

        def load_scales(tile, src, queues):
            for q in range(4):
                queues[q].dma_start(tile[32 * q : 32 * q + 4, :].bitcast(I32), src[0, 4 * q : 4 * q + 4, :].bitcast(I32))

        def gather(name, table, entries, count, dtype):
            tile = held.tile([P, count], dtype, name=name, align_bytes=64)
            nc.vector.tensor_copy(tile[:], table[:].indirect(entries[:]))
            return tile

        def gather_halves(name, word_tab, scale_tab, entries, dtype):
            words = held.tile([P, J], dtype, name=name + "_words", align_bytes=64)
            scales = held.tile([P, J], U8, name=name + "_scales", align_bytes=64)
            for h in range(2):
                cols = slice(h * HALF, (h + 1) * HALF)
                part = entries[:, h * HALF // 16 : (h + 1) * HALF // 16]
                nc.vector.tensor_copy(words[:, cols], word_tab[:].indirect(part))
                nc.vector.tensor_copy(scales[:, cols], scale_tab[:].indirect(part))
            return words, scales

        def gather_dealt(name, table, entries, dtype):
            tile = held.tile([P, I], dtype, name=name, align_bytes=64)
            nc.vector.tensor_copy(tile[:].rearrange("p (t m) -> p m t", t=PACK), table[:].indirect(entries[:]))
            return tile

        q_scale_tab = zeroed_scale_tile("q_scale_tab", nc.vector)
        r_scale_tab = zeroed_scale_tile("r_scale_tab", nc.gpsimd)
        v_scale_tab = zeroed_scale_tile("v_scale_tab", nc.gpsimd)

        k_list = load_list("k_list", offs)
        k_scale_tab = held.tile([P, T], U8, name="k_scale_tab", align_bytes=64)
        for q in range(4):
            rows = xk_scales[0, 4 * q : 4 * q + 4, :].bitcast(I32)
            (nc.scalar, nc.sync)[q % 2].dma_start(
                k_scale_tab[32 * q : 32 * q + 32, :].bitcast(I32), rows.unsqueeze(0).broadcast_to([8, 4, T // 4])
            )
        k_word_tab = load_words("k_word_tab", xk_words[0].rearrange("p c r -> p (c r)"), U32, nc.sync)
        q_word_tab = load_words("q_word_tab", xq_words[0], U16, nc.sync)
        load_scales(q_scale_tab, xq_scales, (nc.sync,) * 4)
        q_list = load_list("q_list", offs2)
        r_word_tab = load_words("r_word_tab", xr_words[0].rearrange("p c r -> p (c r)"), U32, nc.sync)
        load_scales(r_scale_tab, xr_scales, (nc.sync,) * 4)
        r_list = load_list("r_list", offs3)
        v_word_tab = load_words("v_word_tab", vs_words[0], U16, nc.sync)
        load_scales(v_scale_tab, vs_scales, (nc.sync,) * 4)
        v_list = load_list("v_list", offs4)
        first_list = load_list("first_list", offs5)
        second_list = load_list("second_list", offs6)

        k_scales = gather_dealt("k_scales", k_scale_tab, k_list, U8)
        k_words = gather_dealt("k_words", k_word_tab, k_list, U32)
        q_words, q_scales = gather_halves("q", q_word_tab, q_scale_tab, q_list, U16)

        def scores(name, words, scales, dtype, h):
            bank = psum.tile([P, PACK, HALF], F32, name=name)
            cols = slice(h * HALF, (h + 1) * HALF)
            for t in range(PACK):
                rows = slice(t * P, (t + 1) * P)
                nc.tensor.matmul_mx(
                    out=bank[:, t, :],
                    lhsT=k_words[:, rows].bitcast(E4M3), lhsT_scale=k_scales[:, rows],
                    rhs=words[:, cols].bitcast(dtype), rhs_scale=scales[:, cols],
                    start=True, stop=True,
                )
            return bank

        s1 = []
        for h in range(2):
            bank = scores("s1_bank%d" % h, q_words, q_scales, E2M1, h)
            tile = held.tile([P, HALF, PACK], F32, name="s1_%d" % h)
            nc.scalar.copy(tile[:], bank[:].rearrange("p t j -> p j t"))
            s1.append(tile)

        r_words, r_scales = gather_halves("r", r_word_tab, r_scale_tab, r_list, U32)

        hid = []
        diffs = held.tile([P, 2, HALF, PACK], F32, name="diffs")
        for h in range(2):
            bank = scores("s2_bank%d" % h, r_words, r_scales, E5M2, h)
            diff = diffs[:, h]
            nc.vector.tensor_tensor(diff, s1[h][:], bank[:].rearrange("p t j -> p j t"), ALU.subtract)
            rounded = held.tile([P, HALF * PACK], BF16, name="hid%d" % h, align_bytes=64)
            nc.scalar.activation(rounded[:], diff.rearrange("p j t -> p (j t)"), ACT.Abs)
            hid.append(rounded)

        v_words = gather("v_words", v_word_tab, v_list, N, U16)
        v_scales = gather("v_scales", v_scale_tab, v_list, N, U8)

        codes_both = held.tile([P, 2, HALF], U32, name="hid_words", tag="v_word_tab", align_bytes=64)
        p_tiles = [held.tile([P, J], F32, name="p%d" % b) for b in range(2)]
        for h in range(2):
            codes = codes_both[:, h]
            scales = held.tile([P, HALF], U8, name="hid_scales%d" % h, align_bytes=64)
            nc.vector.quantize_mx(out=codes.bitcast(E4M3), scales=scales[:], in_=hid[h][:])
            for b in range(2):
                rows = slice(b * P, (b + 1) * P)
                bank = psum.tile([P, HALF], F32, name="p_bank%d%d" % (h, b))
                nc.tensor.matmul_mx(
                    out=bank[:],
                    lhsT=v_words[:, rows].bitcast(E2M1), lhsT_scale=v_scales[:, rows],
                    rhs=codes.bitcast(E4M3), rhs_scale=scales[:],
                    start=True, stop=True,
                )
                dst = p_tiles[b][:, h * HALF : (h + 1) * HALF]
                if b == 1:
                    nc.vector.tensor_copy(dst, bank[:])
                else:
                    nc.scalar.copy(dst, bank[:])

        picked = []
        for b in range(2):
            first = held.tile([P, E], F32, name="first%d" % b)
            second = held.tile([P, E], F32, name="second%d" % b)
            for tile, entries in ((first, first_list), (second, second_list)):
                if b == 1:
                    nc.vector.tensor_copy(tile[:], p_tiles[b][:].indirect(entries[:]))
                else:
                    nc.scalar.activation(tile[:], p_tiles[b][:].indirect(entries[:]), ACT.Copy)
            picked.append((first, second))
        for b in (1, 0):
            best = held.tile([P, E], F32, name="best%d" % b)
            nc.vector.tensor_tensor(best[:], picked[b][0][:], picked[b][1][:], ALU.max)
            nc.sync.dma_start(out[b * P : (b + 1) * P, :], best[:])
